import numpy as np
import ml_dtypes


def mxq(x, axis, fmt="e4m3"):
    dtype, down = {"e4m3": (ml_dtypes.float8_e4m3fn, 7), "e5m2": (ml_dtypes.float8_e5m2, 14)}[fmt]
    v = np.moveaxis(np.asarray(x, np.float32).astype(ml_dtypes.bfloat16).astype(np.float64), axis, -1)
    blocks = v.reshape(v.shape[:-1] + (-1, 32))
    amax = np.abs(blocks).max(-1, keepdims=True)
    byte = np.maximum(np.where(amax > 0, np.frexp(amax)[1] - 1 + 127, 0) - down, 1)
    scale = np.exp2(byte - 127.0)
    codes = (blocks / scale).astype(np.float32).astype(dtype).astype(np.float64)
    return np.moveaxis((codes * scale).reshape(v.shape), -1, axis)


WIDE = False


def mx_kscale(k):
    if not WIDE:
        return np.ones(k)
    levels = np.array([10, -10, 5, -5, 0])
    if k % 512:
        return np.exp2(np.random.permutation(np.resize(levels, k // 32))).repeat(32)
    a = np.empty((k // 512, 16))
    for p in range(k // 512):
        a[p, :8] = np.random.permutation(np.resize(levels, 8))
        for g in range(8):
            far = levels[np.abs(levels - a[p, g]) >= 10]
            a[p, g + 8] = far[np.random.randint(len(far))]
    return np.exp2(a.ravel()).repeat(32)


def f64(x):
    return np.asarray(x).astype(np.float64)


def striped(idx):
    return np.tile(idx.reshape(-1, 16).T, (8, 1)).astype(np.uint16)


def unstriped(offs):
    return offs[:16].T.reshape(-1).astype(np.int64)


def silu(v):
    return v / (1.0 + np.exp(-np.maximum(v, -700.0)))


K, T, D, S, V, N = 1024, 1024, 4, 1024, 256, 512


def setup_inputs():
    n = np.random.standard_normal
    s = mx_kscale(K)[:, None]
    return {
        "xT": (n((K, T)) * s).astype(np.float32),
        "w": (n((D, K, N)) / np.sqrt(D * K) / s[None]).astype(np.float32),
        "b": (0.3 * n((N, 1))).astype(np.float32),
        "gate": np.tile(np.random.uniform(0.2, 1.0, S), (N, 1)).astype(np.float32),
        "offs": striped(np.random.permutation(T)[:S]),
    }


def reference(xT, w, b, gate, offs):
    idx = unstriped(offs)
    xq = mxq(f64(xT)[:, idx], 0, "e4m3")
    wq = mxq(f64(w), 1, "e4m3")
    y = sum(wq[d].T @ xq[:, d * V:(d + 1) * V] for d in range(D))
    y = silu(y + f64(b))
    out = np.zeros((N, T))
    out[:, idx] = f64(gate) * np.tile(y, (1, D))
    return out

@@ -1,0 +1,185 @@
+from contextlib import ExitStack
+
+import concourse.mybir as mybir
+
+K, T, D, V, N = 1024, 1024, 4, 256, 512
+FLOPS = 2 * K * V * D * N
+
+F32 = mybir.dt.float32
+BF16 = mybir.dt.bfloat16
+U32 = mybir.dt.uint32
+U16 = mybir.dt.uint16
+U8 = mybir.dt.uint8
+FP8X4 = mybir.dt.float8_e4m3fn_x4
+ACT = mybir.ActivationFunctionType
+MULT = mybir.AluOpType.mult
+
+P = 128
+J = 4
+KP = P * J
+A = K // KP
+HALF = T // 2
+XV = [352,352,128,288]
+WBLOCKS = ((0, 128), (128, 128), (256, 256))
+
+
+def lay(dst, src):
+    return dst.rearrange("p (q i) j -> p q j i", i=4), src.rearrange("p j (q i) -> p q j i", i=4)
+
+
+def tile_picked_tome_lin_silu_sub_e_kernel(tc, xT, w, b, gate, offs, out):
+    nc = tc.nc
+    with ExitStack() as ctx:
+        keep = ctx.enter_context(tc.tile_pool(name="keep", bufs=1))
+        ring = ctx.enter_context(tc.tile_pool(name="ring", bufs=4))
+        psum = ctx.enter_context(tc.psum_pool(name="psum", bufs=1))
+
+        offsets = keep.tile([P, T // 16], U16, name="offsets")
+        bias = keep.tile([P, N // P], F32, name="bias")
+        dummy = keep.tile([P, 1], F32, name="dummy")
+        x_scales = keep.tile([P, T], U8, name="x_scales", align_bytes=64)
+        g_scales = keep.tile([P, T], U8, name="g_scales", align_bytes=64)
+        x_words = [keep.tile([P, T], U32, name=f"x_words{a}", align_bytes=64) for a in range(A)]
+        g_words = [keep.tile([P, T], U32, name=f"g_words{a}", align_bytes=64) for a in range(A)]
+
+        x_raw = {}
+        for a in range(A):
+            for h in range(2):
+                raw = keep.tile([P, J, HALF], F32, name=f"x_raw{a}{h}")
+                nc.sync.dma_start(
+                    out=raw[:],
+                    in_=xT[a * KP : (a + 1) * KP, h * HALF : (h + 1) * HALF].rearrange("(p j) c -> p j c", j=J),
+                )
+                x_raw[a, h] = raw
+                if a == 0 and h == 0:
+                    nc.sync.dma_start(offsets[:], offs)
+        with nc.allow_non_contiguous_dma(reason="bias"):
+            nc.scalar.dma_start(out=bias[:], in_=b.rearrange("(m p) o -> p (m o)", p=P))
+        nc.gpsimd.memset(x_scales[:], 0)
+        nc.vector.memset(dummy[:], 0.0)
+        nc.scalar.activation(dummy[:], dummy[:], ACT.Silu)
+
+        gates = [keep.tile([P, T], F32, name=f"gate{m}") for m in range(N // P)]
+        w_raw = {}
+        for i, (c0, width) in enumerate(WBLOCKS):
+            for d in range(D):
+                raw = keep.tile([P, J, A, width], F32, name=f"w_raw{i}{d}")
+                for a in range(A):
+                    nc.sync.dma_start(
+                        out=raw[:, :, a, :],
+                        in_=w[d, a * KP : (a + 1) * KP, c0 : c0 + width].rearrange("(p j) c -> p j c", j=J),
+                    )
+                w_raw[i, d] = raw
+            for m in range(c0 // P, (c0 + width) // P):
+                nc.sync.dma_start(out=gates[m][:], in_=gate[m * P : (m + 1) * P, :])
+
+        for a in range(A):
+            for h in range(2):
+                grouped = keep.tile([P, HALF, J], BF16, name=f"x_grouped{a}{h}", align_bytes=64)
+                s = XV[2 * a + h]
+                dst, src = lay(grouped[:, 0:s, :], x_raw[a, h][:, :, 0:s])
+                nc.vector.tensor_copy(out=dst, in_=src)
+                dst, src = lay(grouped[:, s:HALF, :], x_raw[a, h][:, :, s:HALF])
+                nc.scalar.copy(out=dst, in_=src)
+                cols = slice(h * HALF, (h + 1) * HALF)
+                nc.vector.quantize_mx(
+                    out=x_words[a][:, cols].bitcast(FP8X4),
+                    scales=x_scales[4 * a : P, cols],
+                    in_=grouped[:].rearrange("p c j -> p (c j)"),
+                )
+            for h in range(2):
+                cols = slice(h * HALF, (h + 1) * HALF)
+                nc.vector.tensor_copy(
+                    out=g_words[a][:, cols],
+                    in_=x_words[a][:].indirect(offsets[:, h * HALF // 16 : (h + 1) * HALF // 16]),
+                )
+        for h in range(2):
+            cols = slice(h * HALF, (h + 1) * HALF)
+            nc.vector.tensor_copy(
+                out=g_scales[:, cols],
+                in_=x_scales[:].indirect(offsets[:, h * HALF // 16 : (h + 1) * HALF // 16]),
+            )
+
+        w_codes = {}
+        w_scales = {}
+
+        def quantize_w(i, d):
+            width = WBLOCKS[i][1]
+            cols = A * width
+            grouped = ring.tile([P, cols, J], BF16, name=f"w_grouped_{width}", align_bytes=64)
+            dst, src = lay(grouped[:], w_raw[i, d][:].rearrange("p j a c -> p j (a c)"))
+            nc.scalar.copy(out=dst, in_=src)
+            codes = keep.tile([P, cols], U32, name=f"w_codes{i}{d}", align_bytes=64)
+            scales = keep.tile([P, cols], U8, name=f"w_scales{i}{d}", align_bytes=64)
+            nc.vector.quantize_mx(
+                out=codes[:].bitcast(FP8X4), scales=scales[:], in_=grouped[:].rearrange("p c j -> p (c j)")
+            )
+            w_codes[i, d] = codes
+            w_scales[i, d] = scales
+
+        def multiply(i, m):
+            c0, width = WBLOCKS[i]
+            acc = psum.tile([P, V], F32, name=f"acc{m}")
+            for d in range(D):
+                for a in range(A):
+                    lo = a * width + m * P - c0
+                    nc.tensor.matmul_mx(
+                        out=acc[:],
+                        lhsT=w_codes[i, d][:, lo : lo + P].bitcast(FP8X4),
+                        lhsT_scale=w_scales[i, d][:, lo : lo + P],
+                        rhs=g_words[a][:, d * V : (d + 1) * V].bitcast(FP8X4),
+                        rhs_scale=g_scales[4 * a : P, d * V : (d + 1) * V],
+                        start=(d == 0 and a == 0),
+                        stop=(d == D - 1 and a == A - 1),
+                    )
+            y = keep.tile([P, 2 * V], F32, name=f"y{m}")
+            for r in range(2):
+                nc.scalar.activation(y[:, r * V : (r + 1) * V], acc[:], ACT.Silu, bias=bias[:, m : m + 1])
+            return y
+
+        windows = [keep.tile([P, T], F32, name=f"window{m}") for m in range(N // P)]
+        weighted = [keep.tile([P, T], F32, name=f"weighted{m}") for m in range(N // P)]
+
+        def scatter(m, y, h):
+            cols = slice(h * HALF, (h + 1) * HALF)
+            offs_h = offsets[:, h * HALF // 16 : (h + 1) * HALF // 16]
+            nc.vector.tensor_copy(windows[m][:].indirect(offs_h), weighted[m][:, cols])
+
+        def weigh(m, y):
+            for h in range(2):
+                cols = slice(h * HALF, (h + 1) * HALF)
+                nc.vector.tensor_tensor(weighted[m][:, cols], y[:], gates[m][:, cols], MULT)
+
+        def store(m):
+            nc.sync.dma_start(out=out[m * P : (m + 1) * P, :], in_=windows[m][:])
+
+        for d in range(D):
+            quantize_w(0, d)
+        y0 = multiply(0, 0)
+        weigh(0, y0)
+        scatter(0, y0, 0)
+        for d in range(2):
+            quantize_w(1, d)
+        scatter(0, y0, 1)
+        store(0)
+        for d in range(2, D):
+            quantize_w(1, d)
+        y1 = multiply(1, 1)
+        weigh(1, y1)
+        scatter(1, y1, 0)
+        for d in range(2):
+            quantize_w(2, d)
+        scatter(1, y1, 1)
+        store(1)
+        for d in range(2, D):
+            quantize_w(2, d)
+        y2 = multiply(2, 2)
+        y3 = multiply(2, 3)
+        weigh(2, y2)
+        weigh(3, y3)
+        scatter(2, y2, 0)
+        scatter(3, y3, 0)
+        scatter(2, y2, 1)
+        store(2)
+        scatter(3, y3, 1)
+        store(3)

@@ -18,9 +18,10 @@ P = 128
 J = 4
 KP = P * J
 A = K // KP
+M = N // P
+PAIR = 2
+CHUNKS = ((0,0,512,352),(0,512,512,352),(1,0,512,160),(1,512,256,128),(1,768,256,160))
 HALF = T // 2
-XV = [352,352,128,288]
-WBLOCKS = ((0, 128), (128, 128), (256, 256))
 
 
 def lay(dst, src):
@@ -35,151 +36,165 @@ def tile_picked_tome_lin_silu_sub_e_kernel(tc, xT, w, b, gate, offs, out):
         psum = ctx.enter_context(tc.psum_pool(name="psum", bufs=1))
 
         offsets = keep.tile([P, T // 16], U16, name="offsets")
-        bias = keep.tile([P, N // P], F32, name="bias")
+        bias = keep.tile([P, M], F32, name="bias")
         dummy = keep.tile([P, 1], F32, name="dummy")
         x_scales = keep.tile([P, T], U8, name="x_scales", align_bytes=64)
         g_scales = keep.tile([P, T], U8, name="g_scales", align_bytes=64)
         x_words = [keep.tile([P, T], U32, name=f"x_words{a}", align_bytes=64) for a in range(A)]
         g_words = [keep.tile([P, T], U32, name=f"g_words{a}", align_bytes=64) for a in range(A)]
 
-        x_raw = {}
-        for a in range(A):
-            for h in range(2):
-                raw = keep.tile([P, J, HALF], F32, name=f"x_raw{a}{h}")
-                nc.sync.dma_start(
-                    out=raw[:],
-                    in_=xT[a * KP : (a + 1) * KP, h * HALF : (h + 1) * HALF].rearrange("(p j) c -> p j c", j=J),
-                )
-                x_raw[a, h] = raw
-                if a == 0 and h == 0:
-                    nc.sync.dma_start(offsets[:], offs)
+        x_raw = []
+        for i, (a, t0, n, v) in enumerate(CHUNKS):
+            raw = keep.tile([P, J, n], F32, name=f"x_raw{i}")
+            nc.sync.dma_start(
+                out=raw[:], in_=xT[a * KP : (a + 1) * KP, t0 : t0 + n].rearrange("(p j) c -> p j c", j=J)
+            )
+            x_raw.append(raw)
+            if i == 0:
+                nc.sync.dma_start(offsets[:], offs)
         with nc.allow_non_contiguous_dma(reason="bias"):
             nc.scalar.dma_start(out=bias[:], in_=b.rearrange("(m p) o -> p (m o)", p=P))
         nc.gpsimd.memset(x_scales[:], 0)
         nc.vector.memset(dummy[:], 0.0)
         nc.scalar.activation(dummy[:], dummy[:], ACT.Silu)
 
-        gates = [keep.tile([P, T], F32, name=f"gate{m}") for m in range(N // P)]
+        gates = {(m, h): keep.tile([P, HALF], F32, name=f"gate{m}{h}") for m in range(M) for h in range(2)}
+
+        def load_gate(m, h):
+            nc.sync.dma_start(
+                out=gates[m, h][:], in_=gate[m * P : (m + 1) * P, h * HALF : (h + 1) * HALF]
+            )
+
         w_raw = {}
-        for i, (c0, width) in enumerate(WBLOCKS):
-            for d in range(D):
-                raw = keep.tile([P, J, A, width], F32, name=f"w_raw{i}{d}")
+
+        def load_w(m, u):
+            raw = keep.tile([P, J, PAIR, A, P], F32, name=f"w_raw{m}{u}")
+            for e in range(PAIR):
+                if m > 1 and u == 0 and e == 1:
+                    load_gate(m - 2, 1)
                 for a in range(A):
                     nc.sync.dma_start(
-                        out=raw[:, :, a, :],
-                        in_=w[d, a * KP : (a + 1) * KP, c0 : c0 + width].rearrange("(p j) c -> p j c", j=J),
+                        out=raw[:, :, e, a, :],
+                        in_=w[PAIR * u + e, a * KP : (a + 1) * KP, m * P : (m + 1) * P].rearrange(
+                            "(p j) c -> p j c", j=J
+                        ),
                     )
-                w_raw[i, d] = raw
-            for m in range(c0 // P, (c0 + width) // P):
-                nc.sync.dma_start(out=gates[m][:], in_=gate[m * P : (m + 1) * P, :])
+            w_raw[m, u] = raw
 
-        for a in range(A):
-            for h in range(2):
-                grouped = keep.tile([P, HALF, J], BF16, name=f"x_grouped{a}{h}", align_bytes=64)
-                s = XV[2 * a + h]
-                dst, src = lay(grouped[:, 0:s, :], x_raw[a, h][:, :, 0:s])
-                nc.vector.tensor_copy(out=dst, in_=src)
-                dst, src = lay(grouped[:, s:HALF, :], x_raw[a, h][:, :, s:HALF])
-                nc.scalar.copy(out=dst, in_=src)
-                cols = slice(h * HALF, (h + 1) * HALF)
-                nc.vector.quantize_mx(
-                    out=x_words[a][:, cols].bitcast(FP8X4),
-                    scales=x_scales[4 * a : P, cols],
-                    in_=grouped[:].rearrange("p c j -> p (c j)"),
-                )
+        load_w(0, 0)
+        load_w(0, 1)
+        load_gate(0, 0)
+        for m in range(1, M):
+            load_w(m, 0)
+            load_w(m, 1)
+            load_gate(m, 0)
+        load_gate(M - 1, 1)
+        load_gate(M - 2, 1)
+
+        def round_w(m, u, e0, ne):
+            cols = ne * A * P
+            grouped = ring.tile([P, cols, J], BF16, name=f"w_grouped{ne}", align_bytes=64)
+            dst, src = lay(grouped[:], w_raw[m, u][:, :, e0 : e0 + ne].rearrange("p j e a c -> p j (e a c)"))
+            nc.scalar.copy(out=dst, in_=src)
+            return grouped
+
+        w_codes = {}
+        w_scales = {}
+        for m in range(M):
+            for u in range(D // PAIR):
+                w_codes[m, u] = keep.tile([P, PAIR * A * P], U32, name=f"w_codes{m}{u}", align_bytes=64)
+                w_scales[m, u] = keep.tile([P, PAIR * A * P], U8, name=f"w_scales{m}{u}", align_bytes=64)
+
+        def quantize_w(m, u, grouped, e0, ne):
+            cols = slice(e0 * A * P, (e0 + ne) * A * P)
+            nc.vector.quantize_mx(
+                out=w_codes[m, u][:, cols].bitcast(FP8X4),
+                scales=w_scales[m, u][:, cols],
+                in_=grouped[:].rearrange("p c j -> p (c j)"),
+            )
+
+        def words(a):
             for h in range(2):
                 cols = slice(h * HALF, (h + 1) * HALF)
                 nc.vector.tensor_copy(
                     out=g_words[a][:, cols],
                     in_=x_words[a][:].indirect(offsets[:, h * HALF // 16 : (h + 1) * HALF // 16]),
                 )
-        for h in range(2):
+
+        def scales(h):
             cols = slice(h * HALF, (h + 1) * HALF)
             nc.vector.tensor_copy(
                 out=g_scales[:, cols],
                 in_=x_scales[:].indirect(offsets[:, h * HALF // 16 : (h + 1) * HALF // 16]),
             )
 
-        w_codes = {}
-        w_scales = {}
-
-        def quantize_w(i, d):
-            width = WBLOCKS[i][1]
-            cols = A * width
-            grouped = ring.tile([P, cols, J], BF16, name=f"w_grouped_{width}", align_bytes=64)
-            dst, src = lay(grouped[:], w_raw[i, d][:].rearrange("p j a c -> p j (a c)"))
-            nc.scalar.copy(out=dst, in_=src)
-            codes = keep.tile([P, cols], U32, name=f"w_codes{i}{d}", align_bytes=64)
-            scales = keep.tile([P, cols], U8, name=f"w_scales{i}{d}", align_bytes=64)
+        grouped_x = []
+        for i, (a, t0, n, v) in enumerate(CHUNKS):
+            grouped = keep.tile([P, n, J], BF16, name=f"x_grouped{i}", align_bytes=64)
+            if v > 0:
+                dst, src = lay(grouped[:, 0:v, :], x_raw[i][:, :, 0:v])
+                nc.vector.tensor_copy(out=dst, in_=src)
+            if v < n:
+                dst, src = lay(grouped[:, v:n, :], x_raw[i][:, :, v:n])
+                nc.scalar.copy(out=dst, in_=src)
+            cols = slice(t0, t0 + n)
             nc.vector.quantize_mx(
-                out=codes[:].bitcast(FP8X4), scales=scales[:], in_=grouped[:].rearrange("p c j -> p (c j)")
+                out=x_words[a][:, cols].bitcast(FP8X4),
+                scales=x_scales[4 * a : P, cols],
+                in_=grouped[:].rearrange("p c j -> p (c j)"),
             )
-            w_codes[i, d] = codes
-            w_scales[i, d] = scales
+            if t0 + n == T:
+                words(a)
+        g0 = [round_w(0, d // PAIR, d % PAIR, 1) for d in range(D)]
+        scales(0)
+        quantize_w(0, 0, g0[0], 0, 1)
+        quantize_w(0, 0, g0[1], 1, 1)
+        scales(1)
+        quantize_w(0, 1, g0[2], 0, 1)
+        quantize_w(0, 1, g0[3], 1, 1)
 
-        def multiply(i, m):
-            c0, width = WBLOCKS[i]
+        ys = [keep.tile([P, 2 * V], F32, name=f"y{m}") for m in range(M)]
+
+        def multiply(m):
             acc = psum.tile([P, V], F32, name=f"acc{m}")
             for d in range(D):
+                u, e = divmod(d, PAIR)
                 for a in range(A):
-                    lo = a * width + m * P - c0
+                    lo = (e * A + a) * P
                     nc.tensor.matmul_mx(
                         out=acc[:],
-                        lhsT=w_codes[i, d][:, lo : lo + P].bitcast(FP8X4),
-                        lhsT_scale=w_scales[i, d][:, lo : lo + P],
+                        lhsT=w_codes[m, u][:, lo : lo + P].bitcast(FP8X4),
+                        lhsT_scale=w_scales[m, u][:, lo : lo + P],
                         rhs=g_words[a][:, d * V : (d + 1) * V].bitcast(FP8X4),
                         rhs_scale=g_scales[4 * a : P, d * V : (d + 1) * V],
                         start=(d == 0 and a == 0),
                         stop=(d == D - 1 and a == A - 1),
                     )
-            y = keep.tile([P, 2 * V], F32, name=f"y{m}")
             for r in range(2):
-                nc.scalar.activation(y[:, r * V : (r + 1) * V], acc[:], ACT.Silu, bias=bias[:, m : m + 1])
-            return y
+                nc.scalar.activation(ys[m][:, r * V : (r + 1) * V], acc[:], ACT.Silu, bias=bias[:, m : m + 1])
 
-        windows = [keep.tile([P, T], F32, name=f"window{m}") for m in range(N // P)]
-        weighted = [keep.tile([P, T], F32, name=f"weighted{m}") for m in range(N // P)]
+        windows = [keep.tile([P, T], F32, name=f"window{m}") for m in range(M)]
 
-        def scatter(m, y, h):
-            cols = slice(h * HALF, (h + 1) * HALF)
-            offs_h = offsets[:, h * HALF // 16 : (h + 1) * HALF // 16]
-            nc.vector.tensor_copy(windows[m][:].indirect(offs_h), weighted[m][:, cols])
-
-        def weigh(m, y):
-            for h in range(2):
-                cols = slice(h * HALF, (h + 1) * HALF)
-                nc.vector.tensor_tensor(weighted[m][:, cols], y[:], gates[m][:, cols], MULT)
+        def scatter(m, h):
+            nc.vector.tensor_tensor(
+                windows[m][:].indirect(offsets[:, h * HALF // 16 : (h + 1) * HALF // 16]),
+                ys[m][:],
+                gates[m, h][:],
+                MULT,
+            )
 
         def store(m):
             nc.sync.dma_start(out=out[m * P : (m + 1) * P, :], in_=windows[m][:])
 
-        for d in range(D):
-            quantize_w(0, d)
-        y0 = multiply(0, 0)
-        weigh(0, y0)
-        scatter(0, y0, 0)
-        for d in range(2):
-            quantize_w(1, d)
-        scatter(0, y0, 1)
-        store(0)
-        for d in range(2, D):
-            quantize_w(1, d)
-        y1 = multiply(1, 1)
-        weigh(1, y1)
-        scatter(1, y1, 0)
-        for d in range(2):
-            quantize_w(2, d)
-        scatter(1, y1, 1)
-        store(1)
-        for d in range(2, D):
-            quantize_w(2, d)
-        y2 = multiply(2, 2)
-        y3 = multiply(2, 3)
-        weigh(2, y2)
-        weigh(3, y3)
-        scatter(2, y2, 0)
-        scatter(3, y3, 0)
-        scatter(2, y2, 1)
-        store(2)
-        scatter(3, y3, 1)
-        store(3)
+        multiply(0)
+        scatter(0, 0)
+        for m in range(1, M):
+            quantize_w(m, 0, round_w(m, 0, 0, PAIR), 0, PAIR)
+            for e in range(PAIR):
+                quantize_w(m, 1, round_w(m, 1, e, 1), e, 1)
+            multiply(m)
+            scatter(m - 1, 1)
+            store(m - 1)
+            scatter(m, 0)
+        scatter(M - 1, 1)
+        store(M - 1)

@@ -20,7 +20,7 @@ KP = P * J
 A = K // KP
 M = N // P
 PAIR = 2
-CHUNKS = ((0,0,512,352),(0,512,512,352),(1,0,512,160),(1,512,256,128),(1,768,256,160))
+GROUPS = ((0,0,((256,256),(256,128))),(0,512,((256,128),(256,64))),(1,0,((256,0),(256,0))),(1,512,((256,0),)),(1,768,((256,64),)))
 HALF = T // 2
 
 
@@ -43,15 +43,17 @@ def tile_picked_tome_lin_silu_sub_e_kernel(tc, xT, w, b, gate, offs, out):
         x_words = [keep.tile([P, T], U32, name=f"x_words{a}", align_bytes=64) for a in range(A)]
         g_words = [keep.tile([P, T], U32, name=f"g_words{a}", align_bytes=64) for a in range(A)]
 
-        x_raw = []
-        for i, (a, t0, n, v) in enumerate(CHUNKS):
-            raw = keep.tile([P, J, n], F32, name=f"x_raw{i}")
-            nc.sync.dma_start(
-                out=raw[:], in_=xT[a * KP : (a + 1) * KP, t0 : t0 + n].rearrange("(p j) c -> p j c", j=J)
-            )
-            x_raw.append(raw)
-            if i == 0:
-                nc.sync.dma_start(offsets[:], offs)
+        x_raw = {}
+        for a, t0, parts in GROUPS:
+            for n, v in parts:
+                raw = keep.tile([P, J, n], F32, name=f"x_raw{a}_{t0}")
+                nc.sync.dma_start(
+                    out=raw[:], in_=xT[a * KP : (a + 1) * KP, t0 : t0 + n].rearrange("(p j) c -> p j c", j=J)
+                )
+                x_raw[a, t0] = raw
+                if a == 0 and t0 == 0:
+                    nc.sync.dma_start(offsets[:], offs)
+                t0 += n
         with nc.allow_non_contiguous_dma(reason="bias"):
             nc.scalar.dma_start(out=bias[:], in_=b.rearrange("(m p) o -> p (m o)", p=P))
         nc.gpsimd.memset(x_scales[:], 0)
@@ -91,11 +93,12 @@ def tile_picked_tome_lin_silu_sub_e_kernel(tc, xT, w, b, gate, offs, out):
         load_gate(M - 1, 1)
         load_gate(M - 2, 1)
 
-        def round_w(m, u, e0, ne):
-            cols = ne * A * P
-            grouped = ring.tile([P, cols, J], BF16, name=f"w_grouped{ne}", align_bytes=64)
-            dst, src = lay(grouped[:], w_raw[m, u][:, :, e0 : e0 + ne].rearrange("p j e a c -> p j (e a c)"))
-            nc.scalar.copy(out=dst, in_=src)
+        def round_w(m, u):
+            grouped = ring.tile([P, PAIR * A * P, J], BF16, name="w_grouped", align_bytes=64)
+            for e in range(PAIR):
+                cols = slice(e * A * P, (e + 1) * A * P)
+                dst, src = lay(grouped[:, cols, :], w_raw[m, u][:, :, e].rearrange("p j a c -> p j (a c)"))
+                nc.scalar.copy(out=dst, in_=src)
             return grouped
 
         w_codes = {}
@@ -105,11 +108,10 @@ def tile_picked_tome_lin_silu_sub_e_kernel(tc, xT, w, b, gate, offs, out):
                 w_codes[m, u] = keep.tile([P, PAIR * A * P], U32, name=f"w_codes{m}{u}", align_bytes=64)
                 w_scales[m, u] = keep.tile([P, PAIR * A * P], U8, name=f"w_scales{m}{u}", align_bytes=64)
 
-        def quantize_w(m, u, grouped, e0, ne):
-            cols = slice(e0 * A * P, (e0 + ne) * A * P)
+        def quantize_w(m, u, grouped):
             nc.vector.quantize_mx(
-                out=w_codes[m, u][:, cols].bitcast(FP8X4),
-                scales=w_scales[m, u][:, cols],
+                out=w_codes[m, u][:].bitcast(FP8X4),
+                scales=w_scales[m, u][:],
                 in_=grouped[:].rearrange("p c j -> p (c j)"),
             )
 
@@ -128,30 +130,32 @@ def tile_picked_tome_lin_silu_sub_e_kernel(tc, xT, w, b, gate, offs, out):
                 in_=x_scales[:].indirect(offsets[:, h * HALF // 16 : (h + 1) * HALF // 16]),
             )
 
-        grouped_x = []
-        for i, (a, t0, n, v) in enumerate(CHUNKS):
-            grouped = keep.tile([P, n, J], BF16, name=f"x_grouped{i}", align_bytes=64)
-            if v > 0:
-                dst, src = lay(grouped[:, 0:v, :], x_raw[i][:, :, 0:v])
-                nc.vector.tensor_copy(out=dst, in_=src)
-            if v < n:
-                dst, src = lay(grouped[:, v:n, :], x_raw[i][:, :, v:n])
-                nc.scalar.copy(out=dst, in_=src)
-            cols = slice(t0, t0 + n)
+        for a, t0, parts in GROUPS:
+            total = sum(n for n, v in parts)
+            grouped = keep.tile([P, total, J], BF16, name=f"x_grouped{a}_{t0}", align_bytes=64)
+            c0 = 0
+            for n, v in parts:
+                raw = x_raw[a, t0 + c0]
+                if v > 0:
+                    dst, src = lay(grouped[:, c0 : c0 + v, :], raw[:, :, 0:v])
+                    nc.vector.tensor_copy(out=dst, in_=src)
+                if v < n:
+                    dst, src = lay(grouped[:, c0 + v : c0 + n, :], raw[:, :, v:n])
+                    nc.scalar.copy(out=dst, in_=src)
+                c0 += n
+            cols = slice(t0, t0 + total)
             nc.vector.quantize_mx(
                 out=x_words[a][:, cols].bitcast(FP8X4),
                 scales=x_scales[4 * a : P, cols],
                 in_=grouped[:].rearrange("p c j -> p (c j)"),
             )
-            if t0 + n == T:
+            if t0 + total == T:
                 words(a)
-        g0 = [round_w(0, d // PAIR, d % PAIR, 1) for d in range(D)]
+        g0 = [round_w(0, u) for u in range(D // PAIR)]
         scales(0)
-        quantize_w(0, 0, g0[0], 0, 1)
-        quantize_w(0, 0, g0[1], 1, 1)
+        quantize_w(0, 0, g0[0])
         scales(1)
-        quantize_w(0, 1, g0[2], 0, 1)
-        quantize_w(0, 1, g0[3], 1, 1)
+        quantize_w(0, 1, g0[1])
 
         ys = [keep.tile([P, 2 * V], F32, name=f"y{m}") for m in range(M)]
 
@@ -189,9 +193,8 @@ def tile_picked_tome_lin_silu_sub_e_kernel(tc, xT, w, b, gate, offs, out):
         multiply(0)
         scatter(0, 0)
         for m in range(1, M):
-            quantize_w(m, 0, round_w(m, 0, 0, PAIR), 0, PAIR)
-            for e in range(PAIR):
-                quantize_w(m, 1, round_w(m, 1, e, 1), e, 1)
+            for u in range(D // PAIR):
+                quantize_w(m, u, round_w(m, u))
             multiply(m)
             scatter(m - 1, 1)
             store(m - 1)

@@ -20,7 +20,7 @@ KP = P * J
 A = K // KP
 M = N // P
 PAIR = 2
-GROUPS = ((0,0,((256,256),(256,128))),(0,512,((256,128),(256,64))),(1,0,((256,0),(256,0))),(1,512,((256,0),)),(1,768,((256,64),)))
+GROUPS = ((0,0,((256,256),(256,128))),(0,512,((256,128),(256,128))),(1,0,((256,0),(256,0))),(1,512,((256,0),)),(1,768,((256,64),)))
 HALF = T // 2
 
 
@@ -54,8 +54,6 @@ def tile_picked_tome_lin_silu_sub_e_kernel(tc, xT, w, b, gate, offs, out):
                 if a == 0 and t0 == 0:
                     nc.sync.dma_start(offsets[:], offs)
                 t0 += n
-        with nc.allow_non_contiguous_dma(reason="bias"):
-            nc.scalar.dma_start(out=bias[:], in_=b.rearrange("(m p) o -> p (m o)", p=P))
         nc.gpsimd.memset(x_scales[:], 0)
         nc.vector.memset(dummy[:], 0.0)
         nc.scalar.activation(dummy[:], dummy[:], ACT.Silu)
@@ -69,26 +67,34 @@ def tile_picked_tome_lin_silu_sub_e_kernel(tc, xT, w, b, gate, offs, out):
 
         w_raw = {}
 
-        def load_w(m, u):
-            raw = keep.tile([P, J, PAIR, A, P], F32, name=f"w_raw{m}{u}")
-            for e in range(PAIR):
-                if m > 1 and u == 0 and e == 1:
-                    load_gate(m - 2, 1)
-                for a in range(A):
-                    nc.sync.dma_start(
-                        out=raw[:, :, e, a, :],
-                        in_=w[PAIR * u + e, a * KP : (a + 1) * KP, m * P : (m + 1) * P].rearrange(
-                            "(p j) c -> p j c", j=J
-                        ),
-                    )
-            w_raw[m, u] = raw
+        def load_w(m, d):
+            u, e = divmod(d, PAIR)
+            if e == 0:
+                w_raw[m, u] = keep.tile([P, J, PAIR, A, P], F32, name=f"w_raw{m}{u}")
+            for a in range(A):
+                nc.sync.dma_start(
+                    out=w_raw[m, u][:, :, e, a, :],
+                    in_=w[d, a * KP : (a + 1) * KP, m * P : (m + 1) * P].rearrange("(p j) c -> p j c", j=J),
+                )
 
-        load_w(0, 0)
-        load_w(0, 1)
+        def load_bias():
+            with nc.allow_non_contiguous_dma(reason="bias"):
+                nc.sync.dma_start(out=bias[:], in_=b.rearrange("(m p) o -> p (m o)", p=P))
+
+        for d in range(D):
+            load_w(0, d)
+        load_w(1, 0)
+        load_w(1, 1)
+        load_bias()
+        load_w(1, 2)
         load_gate(0, 0)
-        for m in range(1, M):
+        load_w(1, 3)
+        load_gate(1, 0)
+        for m in range(2, M):
             load_w(m, 0)
-            load_w(m, 1)
+            load_gate(m - 2, 1)
+            for d in range(1, D):
+                load_w(m, d)
             load_gate(m, 0)
         load_gate(M - 1, 1)
         load_gate(M - 2, 1)
@@ -108,11 +114,12 @@ def tile_picked_tome_lin_silu_sub_e_kernel(tc, xT, w, b, gate, offs, out):
                 w_codes[m, u] = keep.tile([P, PAIR * A * P], U32, name=f"w_codes{m}{u}", align_bytes=64)
                 w_scales[m, u] = keep.tile([P, PAIR * A * P], U8, name=f"w_scales{m}{u}", align_bytes=64)
 
-        def quantize_w(m, u, grouped):
+        def quantize_w(m, u, grouped, e0=0, ne=PAIR):
+            cols = slice(e0 * A * P, (e0 + ne) * A * P)
             nc.vector.quantize_mx(
-                out=w_codes[m, u][:].bitcast(FP8X4),
-                scales=w_scales[m, u][:],
-                in_=grouped[:].rearrange("p c j -> p (c j)"),
+                out=w_codes[m, u][:, cols].bitcast(FP8X4),
+                scales=w_scales[m, u][:, cols],
+                in_=grouped[:, cols, :].rearrange("p c j -> p (c j)"),
             )
 
         def words(a):
@@ -155,7 +162,10 @@ def tile_picked_tome_lin_silu_sub_e_kernel(tc, xT, w, b, gate, offs, out):
         scales(0)
         quantize_w(0, 0, g0[0])
         scales(1)
-        quantize_w(0, 1, g0[1])
+        for e in range(PAIR):
+            quantize_w(0, 1, g0[1], e, 1)
+        g1 = round_w(1, 0)
+        quantize_w(1, 0, g1)
 
         ys = [keep.tile([P, 2 * V], F32, name=f"y{m}") for m in range(M)]
 
@@ -193,7 +203,7 @@ def tile_picked_tome_lin_silu_sub_e_kernel(tc, xT, w, b, gate, offs, out):
         multiply(0)
         scatter(0, 0)
         for m in range(1, M):
-            for u in range(D // PAIR):
+            for u in range(1 if m == 1 else 0, D // PAIR):
                 quantize_w(m, u, round_w(m, u))
             multiply(m)
             scatter(m - 1, 1)

from contextlib import ExitStack

import concourse.mybir as mybir

K, T, D, V, N = 1024, 1024, 4, 256, 512
FLOPS = 2 * K * V * D * N

F32 = mybir.dt.float32
BF16 = mybir.dt.bfloat16
U32 = mybir.dt.uint32
U16 = mybir.dt.uint16
U8 = mybir.dt.uint8
FP8X4 = mybir.dt.float8_e4m3fn_x4
ACT = mybir.ActivationFunctionType
MULT = mybir.AluOpType.mult

P = 128
J = 4
KP = P * J
A = K // KP
M = N // P
PAIR = 2
GROUPS = ((0,0,((256,256),(256,128))),(0,512,((256,128),(256,128))),(1,0,((256,0),(256,0))),(1,512,((256,0),)),(1,768,((256,64),)))
HALF = T // 2


def lay(dst, src):
    return dst.rearrange("p (q i) j -> p q j i", i=4), src.rearrange("p j (q i) -> p q j i", i=4)


def tile_picked_tome_lin_silu_sub_e_kernel(tc, xT, w, b, gate, offs, out):
    nc = tc.nc
    with ExitStack() as ctx:
        keep = ctx.enter_context(tc.tile_pool(name="keep", bufs=1))
        ring = ctx.enter_context(tc.tile_pool(name="ring", bufs=4))
        psum = ctx.enter_context(tc.psum_pool(name="psum", bufs=1))

        offsets = keep.tile([P, T // 16], U16, name="offsets")
        bias = keep.tile([P, M], F32, name="bias")
        dummy = keep.tile([P, 1], F32, name="dummy")
        x_scales = keep.tile([P, T], U8, name="x_scales", align_bytes=64)
        g_scales = keep.tile([P, T], U8, name="g_scales", align_bytes=64)
        x_words = [keep.tile([P, T], U32, name=f"x_words{a}", align_bytes=64) for a in range(A)]
        g_words = [keep.tile([P, T], U32, name=f"g_words{a}", align_bytes=64) for a in range(A)]

        x_raw = {}
        for a, t0, parts in GROUPS:
            for n, v in parts:
                raw = keep.tile([P, J, n], F32, name=f"x_raw{a}_{t0}")
                nc.sync.dma_start(
                    out=raw[:], in_=xT[a * KP : (a + 1) * KP, t0 : t0 + n].rearrange("(p j) c -> p j c", j=J)
                )
                x_raw[a, t0] = raw
                if a == 0 and t0 == 0:
                    nc.sync.dma_start(offsets[:], offs)
                t0 += n
        nc.gpsimd.memset(x_scales[:], 0)
        nc.vector.memset(dummy[:], 0.0)
        nc.scalar.activation(dummy[:], dummy[:], ACT.Silu)

        gates = {(m, h): keep.tile([P, HALF], F32, name=f"gate{m}{h}") for m in range(M) for h in range(2)}

        def load_gate(m, h):
            nc.sync.dma_start(
                out=gates[m, h][:], in_=gate[m * P : (m + 1) * P, h * HALF : (h + 1) * HALF]
            )

        w_raw = {}

        def load_w(m, d):
            u, e = divmod(d, PAIR)
            if e == 0:
                w_raw[m, u] = keep.tile([P, J, PAIR, A, P], F32, name=f"w_raw{m}{u}")
            for a in range(A):
                nc.sync.dma_start(
                    out=w_raw[m, u][:, :, e, a, :],
                    in_=w[d, a * KP : (a + 1) * KP, m * P : (m + 1) * P].rearrange("(p j) c -> p j c", j=J),
                )

        def load_bias():
            with nc.allow_non_contiguous_dma(reason="bias"):
                nc.sync.dma_start(out=bias[:], in_=b.rearrange("(m p) o -> p (m o)", p=P))

        for d in range(D):
            load_w(0, d)
        load_w(1, 0)
        load_w(1, 1)
        load_bias()
        load_w(1, 2)
        load_gate(0, 0)
        load_w(1, 3)
        load_gate(1, 0)
        for m in range(2, M):
            load_w(m, 0)
            load_gate(m - 2, 1)
            for d in range(1, D):
                load_w(m, d)
            load_gate(m, 0)
        load_gate(M - 1, 1)
        load_gate(M - 2, 1)

        def round_w(m, u):
            grouped = ring.tile([P, PAIR * A * P, J], BF16, name="w_grouped", align_bytes=64)
            for e in range(PAIR):
                cols = slice(e * A * P, (e + 1) * A * P)
                dst, src = lay(grouped[:, cols, :], w_raw[m, u][:, :, e].rearrange("p j a c -> p j (a c)"))
                nc.scalar.copy(out=dst, in_=src)
            return grouped

        w_codes = {}
        w_scales = {}
        for m in range(M):
            for u in range(D // PAIR):
                w_codes[m, u] = keep.tile([P, PAIR * A * P], U32, name=f"w_codes{m}{u}", align_bytes=64)
                w_scales[m, u] = keep.tile([P, PAIR * A * P], U8, name=f"w_scales{m}{u}", align_bytes=64)

        def quantize_w(m, u, grouped, e0=0, ne=PAIR):
            cols = slice(e0 * A * P, (e0 + ne) * A * P)
            nc.vector.quantize_mx(
                out=w_codes[m, u][:, cols].bitcast(FP8X4),
                scales=w_scales[m, u][:, cols],
                in_=grouped[:, cols, :].rearrange("p c j -> p (c j)"),
            )

        def words(a):
            for h in range(2):
                cols = slice(h * HALF, (h + 1) * HALF)
                nc.vector.tensor_copy(
                    out=g_words[a][:, cols],
                    in_=x_words[a][:].indirect(offsets[:, h * HALF // 16 : (h + 1) * HALF // 16]),
                )

        def scales(h):
            cols = slice(h * HALF, (h + 1) * HALF)
            nc.vector.tensor_copy(
                out=g_scales[:, cols],
                in_=x_scales[:].indirect(offsets[:, h * HALF // 16 : (h + 1) * HALF // 16]),
            )

        for a, t0, parts in GROUPS:
            total = sum(n for n, v in parts)
            grouped = keep.tile([P, total, J], BF16, name=f"x_grouped{a}_{t0}", align_bytes=64)
            c0 = 0
            for n, v in parts:
                raw = x_raw[a, t0 + c0]
                if v > 0:
                    dst, src = lay(grouped[:, c0 : c0 + v, :], raw[:, :, 0:v])
                    nc.vector.tensor_copy(out=dst, in_=src)
                if v < n:
                    dst, src = lay(grouped[:, c0 + v : c0 + n, :], raw[:, :, v:n])
                    nc.scalar.copy(out=dst, in_=src)
                c0 += n
            cols = slice(t0, t0 + total)
            nc.vector.quantize_mx(
                out=x_words[a][:, cols].bitcast(FP8X4),
                scales=x_scales[4 * a : P, cols],
                in_=grouped[:].rearrange("p c j -> p (c j)"),
            )
            if t0 + total == T:
                words(a)
        g0 = [round_w(0, u) for u in range(D // PAIR)]
        scales(0)
        quantize_w(0, 0, g0[0])
        scales(1)
        for e in range(PAIR):
            quantize_w(0, 1, g0[1], e, 1)
        g1 = round_w(1, 0)
        quantize_w(1, 0, g1)

        ys = [keep.tile([P, 2 * V], F32, name=f"y{m}") for m in range(M)]

        def multiply(m):
            acc = psum.tile([P, V], F32, name=f"acc{m}")
            for d in range(D):
                u, e = divmod(d, PAIR)
                for a in range(A):
                    lo = (e * A + a) * P
                    nc.tensor.matmul_mx(
                        out=acc[:],
                        lhsT=w_codes[m, u][:, lo : lo + P].bitcast(FP8X4),
                        lhsT_scale=w_scales[m, u][:, lo : lo + P],
                        rhs=g_words[a][:, d * V : (d + 1) * V].bitcast(FP8X4),
                        rhs_scale=g_scales[4 * a : P, d * V : (d + 1) * V],
                        start=(d == 0 and a == 0),
                        stop=(d == D - 1 and a == A - 1),
                    )
            for r in range(2):
                nc.scalar.activation(ys[m][:, r * V : (r + 1) * V], acc[:], ACT.Silu, bias=bias[:, m : m + 1])

        windows = [keep.tile([P, T], F32, name=f"window{m}") for m in range(M)]

        def scatter(m, h):
            nc.vector.tensor_tensor(
                windows[m][:].indirect(offsets[:, h * HALF // 16 : (h + 1) * HALF // 16]),
                ys[m][:],
                gates[m, h][:],
                MULT,
            )

        def store(m):
            nc.sync.dma_start(out=out[m * P : (m + 1) * P, :], in_=windows[m][:])

        multiply(0)
        scatter(0, 0)
        for m in range(1, M):
            for u in range(1 if m == 1 else 0, D // PAIR):
                quantize_w(m, u, round_w(m, u))
            multiply(m)
            scatter(m - 1, 1)
            store(m - 1)
            scatter(m, 0)
        scatter(M - 1, 1)
        store(M - 1)
